import numpy as np
import ml_dtypes


def mxq(x, axis, fmt="e4m3"):
    dtype, down = {"e4m3": (ml_dtypes.float8_e4m3fn, 7), "e5m2": (ml_dtypes.float8_e5m2, 14)}[fmt]
    v = np.moveaxis(np.asarray(x, np.float32).astype(ml_dtypes.bfloat16).astype(np.float64), axis, -1)
    blocks = v.reshape(v.shape[:-1] + (-1, 32))
    amax = np.abs(blocks).max(-1, keepdims=True)
    byte = np.maximum(np.where(amax > 0, np.frexp(amax)[1] - 1 + 127, 0) - down, 1)
    scale = np.exp2(byte - 127.0)
    codes = (blocks / scale).astype(np.float32).astype(dtype).astype(np.float64)
    return np.moveaxis((codes * scale).reshape(v.shape), -1, axis)


WIDE = False


def mx_kscale(k):
    if not WIDE:
        return np.ones(k)
    levels = np.array([10, -10, 5, -5, 0])
    if k % 512:
        return np.exp2(np.random.permutation(np.resize(levels, k // 32))).repeat(32)
    a = np.empty((k // 512, 16))
    for p in range(k // 512):
        a[p, :8] = np.random.permutation(np.resize(levels, 8))
        for g in range(8):
            far = levels[np.abs(levels - a[p, g]) >= 10]
            a[p, g + 8] = far[np.random.randint(len(far))]
    return np.exp2(a.ravel()).repeat(32)


BF16 = ml_dtypes.bfloat16


def bf(x):
    return np.asarray(x, np.float32).astype(BF16)


def f64(x):
    return np.asarray(x).astype(np.float64)


E2M1 = np.array([0.0, 0.5, 1.0, 1.5, 2.0, 3.0, 4.0, 6.0, -0.0, -0.5, -1.0, -1.5, -2.0, -3.0, -4.0, -6.0])


def pack_weight(w, fmt):
    k, n = w.shape
    w = f64(bf(w)).reshape(k // 32, 32, n)
    amax = np.abs(w).max(1)
    if fmt == "e4m3":
        byte = np.frexp(amax)[1] - 1 + 127 - 7
    else:
        mant, ex = np.frexp(amax / 6.0)
        byte = np.where(mant > 0.5, ex, ex - 1) + 127
    byte = np.clip(np.where(amax > 0, byte, 1), 1, 254)
    scaled = (w * np.exp2(127.0 - byte)[:, None, :]).reshape(k, n).astype(np.float32)
    by_word = np.ascontiguousarray(scaled.reshape(k // 512, 128, 4, n).transpose(0, 1, 3, 2))
    if fmt == "e4m3":
        words = by_word.astype(ml_dtypes.float8_e4m3fn).view(np.uint8)
    else:
        c = by_word.astype(ml_dtypes.float4_e2m1fn).view(np.uint8) & 0xF
        words = c[..., 0::2] | (c[..., 1::2] << 4)
    return np.ascontiguousarray(words), np.ascontiguousarray(byte.astype(np.uint8).reshape(k // 512, 16, n))


def unpack_weight(words, scales, fmt):
    g, p, n, _ = words.shape
    if fmt == "e4m3":
        vals = np.ascontiguousarray(words).view(ml_dtypes.float8_e4m3fn).astype(np.float64)
    else:
        nib = np.empty((g, p, n, 4), np.uint8)
        nib[..., 0::2] = words & 0xF
        nib[..., 1::2] = words >> 4
        vals = E2M1[nib]
    vals = vals * np.repeat(np.exp2(scales.astype(np.float64) - 127.0), 8, axis=1)[..., None]
    return vals.transpose(0, 1, 3, 2).reshape(g * 512, n)
def pack4(w):
    words, scales = pack_weight(w, "e2m1")
    return words.reshape(words.shape[0], 128, -1), scales


def unpack4(words, scales):
    return unpack_weight(words.reshape(words.shape[0], 128, -1, 2), scales, "e2m1")


def planes(Y):
    n, m = Y.shape
    b = f64(bf(Y)).reshape(n // 32, 32, m)
    amax = np.abs(b).max(1)
    byte = np.clip(np.where(amax > 0, np.frexp(amax)[1] - 1 + 127 - 7, 1), 1, 254)
    codes = (b * np.exp2(127.0 - byte)[:, None, :]).reshape(n, m).astype(np.float32).astype(ml_dtypes.float8_e4m3fn).view(np.uint8)
    words = codes.reshape(n // 512, 128, 4, m).transpose(0, 1, 3, 2)
    return np.ascontiguousarray(words), np.ascontiguousarray(byte.astype(np.uint8).reshape(n // 512, 16, m))


G, U, K, S = 4, 1024, 1024, 512

def setup_inputs():
    randn = np.random.randn
    s = mx_kscale(K)
    t = mx_kscale(S)
    channel = randn(G, U, K) * np.exp(0.4 * randn(G, U, 1))
    precoder = randn(G, K, S) / np.sqrt(K)
    leak = 0.4 * np.square(randn(G, S, S)) / S * (1.0 - np.eye(S))
    power = np.exp(0.5 * randn(G, S))
    precoder_words, precoder_scales = pack4((precoder / s[:, None]).reshape(G * K, S))
    leak_words, leak_scales = pack4((leak / t[:, None]).reshape(G * S, S))
    return {
        "channel": bf(channel * s),
        "precoder_words": precoder_words,
        "precoder_scales": precoder_scales,
        "leak_words": leak_words,
        "leak_scales": leak_scales,
        "power": bf(power * t),
        "noise": bf(0.3 * np.exp(0.5 * randn(G, U))),
        "bandwidth": bf(np.exp(0.8 * randn(G, S))),
    }

def reference(channel, precoder_words, precoder_scales, leak_words, leak_scales, power, noise, bandwidth):
    F = unpack4(precoder_words, precoder_scales).reshape(G, K, S)
    C = unpack4(leak_words, leak_scales).reshape(G, S, S)
    e = mxq(f64(channel), 2, "e4m3") @ F
    e2 = np.square(e)
    r = f64(power)[:, None, :] * e2
    leakage = mxq(r, 2, "e4m3") @ C
    y = f64(bandwidth)[:, None, :] * np.log(1.0 + e2 / (leakage + f64(noise)[:, :, None]))
    Y = y.reshape(G * U, S).T
    words, scales = planes(Y)
    return y, words, scales

@@ -1,0 +1,303 @@
+from contextlib import ExitStack
+
+import concourse.mybir as mybir
+from concourse.masks import make_identity
+
+G, U, K, S = 4, 1024, 1024, 512
+FLOPS = 2 * G * U * S * (K + S)
+
+F32 = mybir.dt.float32
+BF16 = mybir.dt.bfloat16
+I32 = mybir.dt.int32
+U32 = mybir.dt.uint32
+U8 = mybir.dt.uint8
+FP8X4 = mybir.dt.float8_e4m3fn_x4
+FP4X4 = mybir.dt.float4_e2m1fn_x4
+ALU = mybir.AluOpType
+ACT = mybir.ActivationFunctionType
+
+P = 128
+PACK = 4
+K_PASS = P * PACK
+PASSES = K // K_PASS
+TILES = G * U // P
+TILES_PER_CELL = U // P
+CODE_GROUP = 4
+BW_ROW = 32
+
+
+def tile_downlink_leakage_rate_map_k7_kernel(
+    tc, channel, precoder_words, precoder_scales, leak_words, leak_scales, power, noise, bandwidth, out_0, out_1, out_2
+):
+    nc = tc.nc
+    channel_rows = channel.rearrange("b u k -> (b u) k")
+    y_rows = out_0.rearrange("b u j -> (b u) j")
+    code_rows = out_1.rearrange("g p m t -> (g p) (m t)").bitcast(I32)
+    scale_rows = out_2.rearrange("g q m -> (g q) m").bitcast(I32)
+
+    with ExitStack() as ctx:
+        keep = ctx.enter_context(tc.tile_pool(name="keep", bufs=1))
+        work = ctx.enter_context(tc.tile_pool(name="work", bufs=3))
+        psum = ctx.enter_context(tc.psum_pool(name="psum", bufs=1))
+        ctx.enter_context(tc.manual_schedule())
+
+        ident = keep.tile([P, P], F32, name="ident")
+        make_identity(nc, ident[:])
+
+        f_scales = keep.tile([P, G * PASSES * S], U8, name="f_scales", align_bytes=64)
+        c_scales = keep.tile([P, G * S], U8, name="c_scales", align_bytes=64)
+        warm = keep.tile([P, 8], F32, name="warm")
+        rows32 = keep.tile([P, P], F32, name="rows32")
+        nc.vector.memset(warm[:], 1.0)
+        nc.vector.memset(f_scales[:].bitcast(I32), 0)
+        nc.vector.memset(c_scales[:].bitcast(I32), 0)
+        nc.vector.memset(rows32[:], 0.0)
+        warm_out = keep.tile([P, 8], F32, name="warm_out")
+        nc.scalar.activation(out=warm_out[:], in_=warm[:], func=ACT.Ln)
+
+        chan = {}
+
+        def load_channel(i):
+            chan[i] = keep.tile([P, K], BF16, name="chan%d" % i)
+            nc.sync.dma_start(out=chan[i][:], in_=channel_rows[i * P : (i + 1) * P, :])
+
+        f_words = {}
+        c_words = {}
+
+        def load_f_words(b):
+            f_words[b] = keep.tile([P, PASSES, 2 * S], U8, name="f_words%d" % b, align_bytes=64)
+            nc.sync.dma_start(
+                out=f_words[b][:].bitcast(I32),
+                in_=precoder_words[PASSES * b : PASSES * (b + 1)].bitcast(I32).rearrange("g p n -> p g n"),
+            )
+
+        def load_c_words(b):
+            c_words[b] = keep.tile([P, 2 * S], U8, name="c_words%d" % b, align_bytes=64)
+            nc.sync.dma_start(out=c_words[b][:].bitcast(I32), in_=leak_words[b].bitcast(I32))
+
+        def load_scales(plane, src):
+            groups = src.shape[0]
+            for q in range(4):
+                nc.sync.dma_start(
+                    out=plane[32 * q : 32 * q + 4, :].bitcast(I32).rearrange("r (g n) -> r g n", g=groups),
+                    in_=src[:, 4 * q : 4 * q + 4, :].bitcast(I32).rearrange("g r n -> r g n"),
+                )
+
+        rows16 = keep.tile([P, P], BF16, name="rows16")
+        power_t = keep.tile([P, G, PACK], BF16, name="power_t")
+
+        load_channel(0)
+        load_f_words(0)
+        load_channel(1)
+        load_scales(f_scales, precoder_scales)
+        load_channel(2)
+        nc.sync.dma_start(out=power_t[:], in_=power.rearrange("b (p t) -> p b t", t=PACK))
+        nc.sync.dma_start(out=rows16[0:TILES, :], in_=noise.rearrange("b (i p) -> (b i) p", p=P))
+        nc.sync.dma_start(out=rows16[BW_ROW : BW_ROW + G * PACK, :], in_=bandwidth.rearrange("b (c p) -> (b c) p", p=P))
+        load_c_words(0)
+        load_scales(c_scales, leak_scales)
+        for i in range(3, TILES):
+            load_channel(i)
+            if i % TILES_PER_CELL == 4 and i // TILES_PER_CELL + 1 < G:
+                load_f_words(i // TILES_PER_CELL + 1)
+                load_c_words(i // TILES_PER_CELL + 1)
+
+        cols = keep.tile([P, 64], F32, name="cols")
+        inv_noise = keep.tile([P, TILES], F32, name="inv_noise")
+        unit = keep.tile([P, TILES], F32, name="unit")
+        safe_noise = keep.tile([P, TILES], F32, name="safe_noise")
+
+        def columns():
+            nc.vector.tensor_copy(out=rows32[0:TILES, :], in_=rows16[0:TILES, :])
+            nc.vector.tensor_copy(out=rows32[BW_ROW : BW_ROW + G * PACK, :], in_=rows16[BW_ROW : BW_ROW + G * PACK, :])
+            bank = psum.tile([P, P], F32, name="cols_bank", tag="yt_bank")
+            nc.tensor.transpose(bank[:], rows32[:], ident[:])
+            nc.vector.tensor_copy(out=cols[:], in_=bank[:, 0:64])
+            nc.vector.scalar_tensor_tensor(
+                out=safe_noise[:], in0=cols[:, 0:TILES], scalar=0.0, in1=cols[:, 0:TILES], op0=ALU.is_equal, op1=ALU.add
+            )
+            nc.vector.reciprocal(out=inv_noise[:], in_=safe_noise[:])
+            nc.vector.tensor_tensor(out=unit[:], in0=cols[:, 0:TILES], in1=inv_noise[:], op=ALU.mult)
+
+        ct_bank, chan_grouped, chan_codes, chan_scales = {}, {}, {}, {}
+        e_bank, e2, et_bank, r_grouped, r_codes, r_scales = {}, {}, {}, {}, {}, {}
+        l_bank, log_den, num, log_num, diff, y, y16 = {}, {}, {}, {}, {}, {}, {}
+        yt_bank, y_grouped, y_codes, y_scales, bw_bank = {}, {}, {}, {}, {}
+
+        def transpose_channel(i):
+            ct_bank[i] = psum.tile([P, PASSES, 2, P], F32, name="ct_bank")
+            words = chan[i][:].bitcast(F32)
+            for g in range(PASSES):
+                for h in range(2):
+                    nc.tensor.transpose(ct_bank[i][:, g, h, :], words[:, 256 * g + h : 256 * (g + 1) : 2], ident[:])
+
+        def copy_channel(i):
+            chan_grouped[i] = work.tile([P, PASSES, P, 2], F32, name="chan_grouped", align_bytes=64)
+            nc.scalar.copy(out=chan_grouped[i][:], in_=ct_bank[i][:].rearrange("p g h u -> p g u h"))
+
+        def quantize_channel(i):
+            chan_codes[i] = work.tile([P, PASSES * P], U32, name="chan_codes", align_bytes=64)
+            chan_scales[i] = work.tile([P, PASSES * P], U8, name="chan_scales", align_bytes=64)
+            nc.vector.quantize_mx(
+                out=chan_codes[i][:].bitcast(FP8X4),
+                scales=chan_scales[i][:],
+                in_=chan_grouped[i][:].rearrange("p g u h -> p (g u h)").bitcast(BF16),
+            )
+
+        def amplitude(i):
+            b = i // TILES_PER_CELL
+            e_bank[i] = psum.tile([P, S], F32, name="e_bank")
+            for g in range(PASSES):
+                group = PASSES * b + g
+                nc.tensor.matmul_mx(
+                    out=e_bank[i][:],
+                    lhsT=chan_codes[i][:, g * P : (g + 1) * P].bitcast(FP8X4),
+                    lhsT_scale=chan_scales[i][:, g * P : (g + 1) * P],
+                    rhs=f_words[b][:, g, :].bitcast(FP4X4),
+                    rhs_scale=f_scales[:, group * S : (group + 1) * S],
+                    start=(g == 0),
+                    stop=(g == PASSES - 1),
+                )
+
+        def square(i):
+            e2[i] = work.tile([P, PACK, P], F32, name="e2", bufs=4)
+            nc.scalar.activation(out=e2[i][:], in_=e_bank[i][:].rearrange("u (p t) -> u t p", t=PACK), func=ACT.Square)
+
+        def transpose_square(i):
+            et_bank[i] = psum.tile([P, PACK, P], F32, name="et_bank", bufs=2)
+            for t in range(PACK):
+                nc.tensor.transpose(et_bank[i][:, t, :], e2[i][:, t, :], ident[:])
+
+        def received(i):
+            b = i // TILES_PER_CELL
+            r_grouped[i] = work.tile([P, P, PACK], BF16, name="r_grouped", align_bytes=64)
+            nc.vector.tensor_tensor(
+                out=r_grouped[i][:],
+                in0=et_bank[i][:].rearrange("p t u -> p u t"),
+                in1=power_t[:, b, :].unsqueeze(1).to_broadcast([P, P, PACK]),
+                op=ALU.mult,
+            )
+
+        def quantize_received(i):
+            r_codes[i] = work.tile([P, P], U32, name="r_codes", align_bytes=64)
+            r_scales[i] = work.tile([P, P], U8, name="r_scales", align_bytes=64)
+            nc.vector.quantize_mx(
+                out=r_codes[i][:].bitcast(FP8X4), scales=r_scales[i][:], in_=r_grouped[i][:].rearrange("p u t -> p (u t)")
+            )
+
+        def leakage(i):
+            b = i // TILES_PER_CELL
+            l_bank[i] = psum.tile([P, S], F32, name="l_bank")
+            nc.tensor.matmul_mx(
+                out=l_bank[i][:],
+                lhsT=r_codes[i][:].bitcast(FP8X4),
+                lhsT_scale=r_scales[i][:],
+                rhs=c_words[b][:].bitcast(FP4X4),
+                rhs_scale=c_scales[:, b * S : (b + 1) * S],
+                start=True,
+                stop=True,
+            )
+
+        def log_denominator(i):
+            log_den[i] = work.tile([P, S], F32, name="log_den")
+            nc.scalar.activation(
+                out=log_den[i][:], in_=l_bank[i][:], func=ACT.Ln, scale=inv_noise[:, i : i + 1], bias=unit[:, i : i + 1]
+            )
+
+        def numerator(i):
+            num[i] = work.tile([P, PACK, P], F32, name="num")
+            nc.vector.tensor_tensor(
+                out=num[i][:], in0=l_bank[i][:].rearrange("u (p t) -> u t p", t=PACK), in1=e2[i][:], op=ALU.add
+            )
+
+        def log_numerator(i):
+            log_num[i] = work.tile([P, PACK, P], F32, name="log_num")
+            nc.scalar.activation(
+                out=log_num[i][:], in_=num[i][:], func=ACT.Ln, scale=inv_noise[:, i : i + 1], bias=unit[:, i : i + 1]
+            )
+
+        def difference(i):
+            diff[i] = work.tile([P, S], F32, name="diff")
+            nc.gpsimd.tensor_tensor(
+                out=diff[i][:].rearrange("u (p t) -> u p t", t=PACK),
+                in0=log_num[i][:].rearrange("u t p -> u p t"),
+                in1=log_den[i][:].rearrange("u (p t) -> u p t", t=PACK),
+                op=ALU.subtract,
+            )
+
+        def spread_bandwidth(b):
+            bw_bank[b] = psum.tile([P, PACK, P], F32, name="bw_bank", bufs=2)
+            for c in range(PACK):
+                col = BW_ROW + PACK * b + c
+                nc.tensor.transpose(bw_bank[b][:, c, :], cols[:, col : col + 1].to_broadcast([P, P]), ident[:])
+
+        def rate(i):
+            b = i // TILES_PER_CELL
+            y[i] = work.tile([P, S], F32, name="y", bufs=6)
+            nc.vector.tensor_tensor(out=y[i][:], in0=diff[i][:], in1=bw_bank[b][:].rearrange("u c p -> u (c p)"), op=ALU.mult)
+            nc.sync.dma_start(out=y_rows[i * P : (i + 1) * P, :], in_=y[i][:])
+
+        def round_rate(i):
+            y16[i] = work.tile([P, 2, P, 2], BF16, name="y16")
+            nc.vector.tensor_copy(out=y16[i][:], in_=y[i][:].rearrange("u (p h e) -> u h p e", h=2, e=2))
+
+        def transpose_rate(i):
+            yt_bank[i] = psum.tile([P, 2, P], F32, name="yt_bank", tag="yt_bank")
+            words = y16[i][:].rearrange("u h p e -> u (h p e)").bitcast(F32)
+            for h in range(2):
+                nc.tensor.transpose(yt_bank[i][:, h, :], words[:, h * P : (h + 1) * P], ident[:])
+
+        def copy_rate(i):
+            y_grouped[i] = work.tile([P, P, 2], F32, name="y_grouped", align_bytes=64)
+            nc.scalar.copy(out=y_grouped[i][:], in_=yt_bank[i][:].rearrange("p h u -> p u h"))
+
+        def quantize_rate(i):
+            group, slot = divmod(i, CODE_GROUP)
+            b, place = divmod(i, TILES_PER_CELL)
+            if slot == 0:
+                y_codes[group] = work.tile([P, CODE_GROUP * P], U32, name="y_codes", align_bytes=64)
+            if place == 0:
+                y_scales[b] = work.tile([P, U], U8, name="y_scales", align_bytes=64)
+            nc.vector.quantize_mx(
+                out=y_codes[group][:, slot * P : (slot + 1) * P].bitcast(FP8X4),
+                scales=y_scales[b][:, place * P : (place + 1) * P],
+                in_=y_grouped[i][:].rearrange("p u h -> p (u h)").bitcast(BF16),
+            )
+            if slot == CODE_GROUP - 1:
+                width = CODE_GROUP * P
+                nc.sync.dma_start(out=code_rows[:, group * width : (group + 1) * width], in_=y_codes[group][:].bitcast(I32))
+            if place == TILES_PER_CELL - 1:
+                for q in range(4):
+                    nc.sync.dma_start(
+                        out=scale_rows[4 * q : 4 * q + 4, b * U // 4 : (b + 1) * U // 4],
+                        in_=y_scales[b][32 * q : 32 * q + 4, :].bitcast(I32),
+                    )
+
+        stages = [
+            (leakage, 3),
+            (amplitude, 1),
+            (log_denominator, 3),
+            (difference, 4),
+            (rate, 5),
+            (received, 2),
+            (square, 1),
+            (numerator, 3),
+            (transpose_channel, 0),
+            (transpose_rate, 6),
+            (transpose_square, 1),
+            (copy_channel, 0),
+            (copy_rate, 6),
+            (log_numerator, 3),
+            (round_rate, 5),
+            (quantize_received, 2),
+            (quantize_channel, 0),
+            (quantize_rate, 6),
+        ]
+        for step in range(TILES + 6):
+            for stage, lag in stages:
+                if 0 <= step - lag < TILES:
+                    stage(step - lag)
+            if step == 1:
+                columns()
+            if (step - 3) % TILES_PER_CELL == 0 and (step - 3) // TILES_PER_CELL < G:
+                spread_bandwidth((step - 3) // TILES_PER_CELL)

@@ -122,10 +122,11 @@ def tile_downlink_leakage_rate_map_k7_kernel(
         ct_bank, chan_grouped, chan_codes, chan_scales = {}, {}, {}, {}
         e_bank, e2, et_bank, r_grouped, r_codes, r_scales = {}, {}, {}, {}, {}, {}
         l_bank, log_den, num, log_num, diff, y, y16 = {}, {}, {}, {}, {}, {}, {}
+        l_twin = {}
         yt_bank, y_grouped, y_codes, y_scales, bw_bank = {}, {}, {}, {}, {}
 
         def transpose_channel(i):
-            ct_bank[i] = psum.tile([P, PASSES, 2, P], F32, name="ct_bank")
+            ct_bank[i] = psum.tile([P, PASSES, 2, P], F32, name="ct_bank", bufs=2)
             words = chan[i][:].bitcast(F32)
             for g in range(PASSES):
                 for h in range(2):
@@ -160,11 +161,11 @@ def tile_downlink_leakage_rate_map_k7_kernel(
                 )
 
         def square(i):
-            e2[i] = work.tile([P, PACK, P], F32, name="e2", bufs=4)
+            e2[i] = work.tile([P, PACK, P], F32, name="e2", bufs=5)
             nc.scalar.activation(out=e2[i][:], in_=e_bank[i][:].rearrange("u (p t) -> u t p", t=PACK), func=ACT.Square)
 
         def transpose_square(i):
-            et_bank[i] = psum.tile([P, PACK, P], F32, name="et_bank", bufs=2)
+            et_bank[i] = psum.tile([P, PACK, P], F32, name="et_bank")
             for t in range(PACK):
                 nc.tensor.transpose(et_bank[i][:, t, :], e2[i][:, t, :], ident[:])
 
@@ -188,15 +189,17 @@ def tile_downlink_leakage_rate_map_k7_kernel(
         def leakage(i):
             b = i // TILES_PER_CELL
             l_bank[i] = psum.tile([P, S], F32, name="l_bank")
-            nc.tensor.matmul_mx(
-                out=l_bank[i][:],
-                lhsT=r_codes[i][:].bitcast(FP8X4),
-                lhsT_scale=r_scales[i][:],
-                rhs=c_words[b][:].bitcast(FP4X4),
-                rhs_scale=c_scales[:, b * S : (b + 1) * S],
-                start=True,
-                stop=True,
-            )
+            l_twin[i] = psum.tile([P, S], F32, name="l_twin")
+            for bank in (l_bank[i], l_twin[i]):
+                nc.tensor.matmul_mx(
+                    out=bank[:],
+                    lhsT=r_codes[i][:].bitcast(FP8X4),
+                    lhsT_scale=r_scales[i][:],
+                    rhs=c_words[b][:].bitcast(FP4X4),
+                    rhs_scale=c_scales[:, b * S : (b + 1) * S],
+                    start=True,
+                    stop=True,
+                )
 
         def log_denominator(i):
             log_den[i] = work.tile([P, S], F32, name="log_den")
@@ -205,28 +208,30 @@ def tile_downlink_leakage_rate_map_k7_kernel(
             )
 
         def numerator(i):
-            num[i] = work.tile([P, PACK, P], F32, name="num")
+            num[i] = work.tile([P, P // 2, PACK, 2], F32, name="num")
             nc.vector.tensor_tensor(
-                out=num[i][:], in0=l_bank[i][:].rearrange("u (p t) -> u t p", t=PACK), in1=e2[i][:], op=ALU.add
+                out=num[i][:],
+                in0=l_twin[i][:].rearrange("u (c e t) -> u c t e", e=2, t=PACK),
+                in1=e2[i][:].rearrange("u t (c e) -> u c t e", e=2),
+                op=ALU.add,
             )
 
         def log_numerator(i):
-            log_num[i] = work.tile([P, PACK, P], F32, name="log_num")
+            log_num[i] = work.tile([P, S], F32, name="log_num")
             nc.scalar.activation(
-                out=log_num[i][:], in_=num[i][:], func=ACT.Ln, scale=inv_noise[:, i : i + 1], bias=unit[:, i : i + 1]
+                out=log_num[i][:].rearrange("u (c e t) -> u c e t", e=2, t=PACK),
+                in_=num[i][:].rearrange("u c t e -> u c e t"),
+                func=ACT.Ln,
+                scale=inv_noise[:, i : i + 1],
+                bias=unit[:, i : i + 1],
             )
 
         def difference(i):
             diff[i] = work.tile([P, S], F32, name="diff")
-            nc.gpsimd.tensor_tensor(
-                out=diff[i][:].rearrange("u (p t) -> u p t", t=PACK),
-                in0=log_num[i][:].rearrange("u t p -> u p t"),
-                in1=log_den[i][:].rearrange("u (p t) -> u p t", t=PACK),
-                op=ALU.subtract,
-            )
+            nc.gpsimd.tensor_tensor(out=diff[i][:], in0=log_num[i][:], in1=log_den[i][:], op=ALU.subtract)
 
         def spread_bandwidth(b):
-            bw_bank[b] = psum.tile([P, PACK, P], F32, name="bw_bank", bufs=2)
+            bw_bank[b] = psum.tile([P, PACK, P], F32, name="bw_bank")
             for c in range(PACK):
                 col = BW_ROW + PACK * b + c
                 nc.tensor.transpose(bw_bank[b][:, c, :], cols[:, col : col + 1].to_broadcast([P, P]), ident[:])
@@ -273,31 +278,36 @@ def tile_downlink_leakage_rate_map_k7_kernel(
                         in_=y_scales[b][32 * q : 32 * q + 4, :].bitcast(I32),
                     )
 
+        def next_bandwidth(i):
+            if (i + 1) % TILES_PER_CELL == 0 and i + 1 < TILES:
+                spread_bandwidth((i + 1) // TILES_PER_CELL)
+
         stages = [
-            (leakage, 3),
-            (amplitude, 1),
-            (log_denominator, 3),
-            (difference, 4),
-            (rate, 5),
-            (received, 2),
-            (square, 1),
-            (numerator, 3),
+            (leakage, 4),
+            (amplitude, 2),
+            (copy_channel, 1),
+            (log_denominator, 4),
+            (difference, 5),
+            (rate, 6),
+            (received, 3),
+            (square, 2),
+            (numerator, 4),
             (transpose_channel, 0),
-            (transpose_rate, 6),
-            (transpose_square, 1),
-            (copy_channel, 0),
-            (copy_rate, 6),
-            (log_numerator, 3),
-            (round_rate, 5),
-            (quantize_received, 2),
-            (quantize_channel, 0),
-            (quantize_rate, 6),
+            (transpose_rate, 7),
+            (next_bandwidth, 6),
+            (transpose_square, 2),
+            (copy_rate, 7),
+            (log_numerator, 4),
+            (quantize_received, 3),
+            (round_rate, 6),
+            (quantize_rate, 7),
+            (quantize_channel, 1),
         ]
-        for step in range(TILES + 6):
+        for step in range(TILES + 7):
             for stage, lag in stages:
                 if 0 <= step - lag < TILES:
                     stage(step - lag)
-            if step == 1:
+            if step == 2:
                 columns()
-            if (step - 3) % TILES_PER_CELL == 0 and (step - 3) // TILES_PER_CELL < G:
-                spread_bandwidth((step - 3) // TILES_PER_CELL)
+            if step == 3:
+                spread_bandwidth(0)

@@ -57,9 +57,13 @@ def tile_downlink_leakage_rate_map_k7_kernel(
 
         chan = {}
 
-        def load_channel(i):
-            chan[i] = keep.tile([P, K], BF16, name="chan%d" % i)
-            nc.sync.dma_start(out=chan[i][:], in_=channel_rows[i * P : (i + 1) * P, :])
+        def load_channel(first, count):
+            rows = keep.tile([P, count, K], BF16, name="chan%d" % first)
+            nc.sync.dma_start(
+                out=rows[:], in_=channel_rows[first * P : (first + count) * P, :].rearrange("(n u) k -> u n k", u=P)
+            )
+            for n in range(count):
+                chan[first + n] = rows[:, n, :]
 
         f_words = {}
         c_words = {}
@@ -86,21 +90,22 @@ def tile_downlink_leakage_rate_map_k7_kernel(
         rows16 = keep.tile([P, P], BF16, name="rows16")
         power_t = keep.tile([P, G, PACK], BF16, name="power_t")
 
-        load_channel(0)
+        load_channel(0, 1)
         load_f_words(0)
-        load_channel(1)
+        load_channel(1, 1)
         load_scales(f_scales, precoder_scales)
-        load_channel(2)
+        load_channel(2, 1)
         nc.sync.dma_start(out=power_t[:], in_=power.rearrange("b (p t) -> p b t", t=PACK))
         nc.sync.dma_start(out=rows16[0:TILES, :], in_=noise.rearrange("b (i p) -> (b i) p", p=P))
         nc.sync.dma_start(out=rows16[BW_ROW : BW_ROW + G * PACK, :], in_=bandwidth.rearrange("b (c p) -> (b c) p", p=P))
         load_c_words(0)
         load_scales(c_scales, leak_scales)
-        for i in range(3, TILES):
-            load_channel(i)
-            if i % TILES_PER_CELL == 4 and i // TILES_PER_CELL + 1 < G:
-                load_f_words(i // TILES_PER_CELL + 1)
-                load_c_words(i // TILES_PER_CELL + 1)
+        load_channel(3, 1)
+        for first in range(4, TILES, 4):
+            load_channel(first, 4)
+            if first % TILES_PER_CELL == 4 and first // TILES_PER_CELL + 1 < G:
+                load_f_words(first // TILES_PER_CELL + 1)
+                load_c_words(first // TILES_PER_CELL + 1)
 
         cols = keep.tile([P, 64], F32, name="cols")
         inv_noise = keep.tile([P, TILES], F32, name="inv_noise")
@@ -110,7 +115,7 @@ def tile_downlink_leakage_rate_map_k7_kernel(
         def columns():
             nc.vector.tensor_copy(out=rows32[0:TILES, :], in_=rows16[0:TILES, :])
             nc.vector.tensor_copy(out=rows32[BW_ROW : BW_ROW + G * PACK, :], in_=rows16[BW_ROW : BW_ROW + G * PACK, :])
-            bank = psum.tile([P, P], F32, name="cols_bank", tag="yt_bank")
+            bank = psum.tile([P, P], F32, name="cols_bank", tag="bw_bank")
             nc.tensor.transpose(bank[:], rows32[:], ident[:])
             nc.vector.tensor_copy(out=cols[:], in_=bank[:, 0:64])
             nc.vector.scalar_tensor_tensor(
@@ -126,8 +131,9 @@ def tile_downlink_leakage_rate_map_k7_kernel(
         yt_bank, y_grouped, y_codes, y_scales, bw_bank = {}, {}, {}, {}, {}
 
         def transpose_channel(i):
-            ct_bank[i] = psum.tile([P, PASSES, 2, P], F32, name="ct_bank", bufs=2)
-            words = chan[i][:].bitcast(F32)
+            tag = "yt_bank" if i % 2 == 1 and i < 7 else "ct_bank"
+            ct_bank[i] = psum.tile([P, PASSES, 2, P], F32, name="ct_bank", tag=tag)
+            words = chan[i].bitcast(F32)
             for g in range(PASSES):
                 for h in range(2):
                     nc.tensor.transpose(ct_bank[i][:, g, h, :], words[:, 256 * g + h : 256 * (g + 1) : 2], ident[:])
@@ -162,10 +168,14 @@ def tile_downlink_leakage_rate_map_k7_kernel(
 
         def square(i):
             e2[i] = work.tile([P, PACK, P], F32, name="e2", bufs=5)
-            nc.scalar.activation(out=e2[i][:], in_=e_bank[i][:].rearrange("u (p t) -> u t p", t=PACK), func=ACT.Square)
+            nc.scalar.activation(
+                out=e2[i][:].rearrange("u t (c n) -> u c t n", n=4),
+                in_=e_bank[i][:].rearrange("u (c n t) -> u c t n", n=4, t=PACK),
+                func=ACT.Square,
+            )
 
         def transpose_square(i):
-            et_bank[i] = psum.tile([P, PACK, P], F32, name="et_bank")
+            et_bank[i] = psum.tile([P, PACK, P], F32, name="et_bank", bufs=2)
             for t in range(PACK):
                 nc.tensor.transpose(et_bank[i][:, t, :], e2[i][:, t, :], ident[:])
 
@@ -231,14 +241,14 @@ def tile_downlink_leakage_rate_map_k7_kernel(
             nc.gpsimd.tensor_tensor(out=diff[i][:], in0=log_num[i][:], in1=log_den[i][:], op=ALU.subtract)
 
         def spread_bandwidth(b):
-            bw_bank[b] = psum.tile([P, PACK, P], F32, name="bw_bank")
+            bw_bank[b] = psum.tile([P, PACK, P], F32, name="bw_bank", tag="bw_bank")
             for c in range(PACK):
                 col = BW_ROW + PACK * b + c
                 nc.tensor.transpose(bw_bank[b][:, c, :], cols[:, col : col + 1].to_broadcast([P, P]), ident[:])
 
         def rate(i):
             b = i // TILES_PER_CELL
-            y[i] = work.tile([P, S], F32, name="y", bufs=6)
+            y[i] = work.tile([P, S], F32, name="y", bufs=TILES)
             nc.vector.tensor_tensor(out=y[i][:], in0=diff[i][:], in1=bw_bank[b][:].rearrange("u c p -> u (c p)"), op=ALU.mult)
             nc.sync.dma_start(out=y_rows[i * P : (i + 1) * P, :], in_=y[i][:])
 
@@ -253,25 +263,30 @@ def tile_downlink_leakage_rate_map_k7_kernel(
                 nc.tensor.transpose(yt_bank[i][:, h, :], words[:, h * P : (h + 1) * P], ident[:])
 
         def copy_rate(i):
-            y_grouped[i] = work.tile([P, P, 2], F32, name="y_grouped", align_bytes=64)
-            nc.scalar.copy(out=y_grouped[i][:], in_=yt_bank[i][:].rearrange("p h u -> p u h"))
+            pair, half = divmod(i, 2)
+            if half == 0:
+                y_grouped[pair] = work.tile([P, 2, P, 2], F32, name="y_grouped", align_bytes=64)
+            nc.scalar.copy(out=y_grouped[pair][:, half], in_=yt_bank[i][:].rearrange("p h u -> p u h"))
 
         def quantize_rate(i):
-            group, slot = divmod(i, CODE_GROUP)
-            b, place = divmod(i, TILES_PER_CELL)
+            if i % 2 == 0:
+                return
+            first = i - 1
+            group, slot = divmod(first, CODE_GROUP)
+            b, place = divmod(first, TILES_PER_CELL)
             if slot == 0:
-                y_codes[group] = work.tile([P, CODE_GROUP * P], U32, name="y_codes", align_bytes=64)
+                y_codes[group] = keep.tile([P, CODE_GROUP * P], U32, name="y_codes%d" % group, align_bytes=64)
             if place == 0:
-                y_scales[b] = work.tile([P, U], U8, name="y_scales", align_bytes=64)
+                y_scales[b] = keep.tile([P, U], U8, name="y_scales%d" % b, align_bytes=64)
             nc.vector.quantize_mx(
-                out=y_codes[group][:, slot * P : (slot + 1) * P].bitcast(FP8X4),
-                scales=y_scales[b][:, place * P : (place + 1) * P],
-                in_=y_grouped[i][:].rearrange("p u h -> p (u h)").bitcast(BF16),
+                out=y_codes[group][:, slot * P : (slot + 2) * P].bitcast(FP8X4),
+                scales=y_scales[b][:, place * P : (place + 2) * P],
+                in_=y_grouped[first // 2][:].rearrange("p n u h -> p (n u h)").bitcast(BF16),
             )
-            if slot == CODE_GROUP - 1:
+            if slot + 2 == CODE_GROUP:
                 width = CODE_GROUP * P
                 nc.sync.dma_start(out=code_rows[:, group * width : (group + 1) * width], in_=y_codes[group][:].bitcast(I32))
-            if place == TILES_PER_CELL - 1:
+            if place + 2 == TILES_PER_CELL:
                 for q in range(4):
                     nc.sync.dma_start(
                         out=scale_rows[4 * q : 4 * q + 4, b * U // 4 : (b + 1) * U // 4],
@@ -283,31 +298,31 @@ def tile_downlink_leakage_rate_map_k7_kernel(
                 spread_bandwidth((i + 1) // TILES_PER_CELL)
 
         stages = [
-            (leakage, 4),
+            (leakage, 5),
+            (square, 3),
+            (log_denominator, 5),
+            (difference, 6),
+            (rate, 7),
+            (received, 4),
+            (numerator, 5),
+            (transpose_rate, 8),
+            (next_bandwidth, 7),
+            (transpose_square, 3),
             (amplitude, 2),
             (copy_channel, 1),
-            (log_denominator, 4),
-            (difference, 5),
-            (rate, 6),
-            (received, 3),
-            (square, 2),
-            (numerator, 4),
             (transpose_channel, 0),
-            (transpose_rate, 7),
-            (next_bandwidth, 6),
-            (transpose_square, 2),
-            (copy_rate, 7),
-            (log_numerator, 4),
-            (quantize_received, 3),
-            (round_rate, 6),
-            (quantize_rate, 7),
+            (copy_rate, 8),
+            (log_numerator, 5),
+            (quantize_received, 4),
+            (round_rate, 7),
+            (quantize_rate, 8),
             (quantize_channel, 1),
         ]
-        for step in range(TILES + 7):
+        for step in range(TILES + 8):
             for stage, lag in stages:
                 if 0 <= step - lag < TILES:
                     stage(step - lag)
             if step == 2:
                 columns()
-            if step == 3:
+            if step == 4:
                 spread_bandwidth(0)

@@ -20,10 +20,14 @@ P = 128
 PACK = 4
 K_PASS = P * PACK
 PASSES = K // K_PASS
+PASS_PAIRS = K_PASS // 2
+QUADRANTS = 4
 TILES = G * U // P
 TILES_PER_CELL = U // P
-CODE_GROUP = 4
-BW_ROW = 32
+LOAD_TILES = 4
+BW_CHUNKS = S // P
+BW_FIRST = TILES
+TABLE_ROWS = BW_FIRST + G * BW_CHUNKS
 
 
 def tile_downlink_leakage_rate_map_k7_kernel(
@@ -44,18 +48,20 @@ def tile_downlink_leakage_rate_map_k7_kernel(
         ident = keep.tile([P, P], F32, name="ident")
         make_identity(nc, ident[:])
 
-        f_scales = keep.tile([P, G * PASSES * S], U8, name="f_scales", align_bytes=64)
+        f_scales_first = keep.tile([P, PASSES * S], U8, name="f_scales_first", align_bytes=64)
+        f_scales_rest = keep.tile([P, (G - 1) * PASSES * S], U8, name="f_scales_rest", align_bytes=64)
         c_scales = keep.tile([P, G * S], U8, name="c_scales", align_bytes=64)
         warm = keep.tile([P, 8], F32, name="warm")
-        rows32 = keep.tile([P, P], F32, name="rows32")
+        table32 = keep.tile([P, P], F32, name="rows32")
         nc.vector.memset(warm[:], 1.0)
-        nc.vector.memset(f_scales[:].bitcast(I32), 0)
+        nc.vector.memset(f_scales_first[:].bitcast(I32), 0)
         nc.vector.memset(c_scales[:].bitcast(I32), 0)
-        nc.vector.memset(rows32[:], 0.0)
+        nc.vector.memset(f_scales_rest[:].bitcast(I32), 0)
+        nc.vector.memset(table32[:], 0.0)
         warm_out = keep.tile([P, 8], F32, name="warm_out")
         nc.scalar.activation(out=warm_out[:], in_=warm[:], func=ACT.Ln)
 
-        chan = {}
+        chan, f_words, c_words = {}, {}, {}
 
         def load_channel(first, count):
             rows = keep.tile([P, count, K], BF16, name="chan%d" % first)
@@ -64,9 +70,6 @@ def tile_downlink_leakage_rate_map_k7_kernel(
             )
             for n in range(count):
                 chan[first + n] = rows[:, n, :]
-
-        f_words = {}
-        c_words = {}
 
         def load_f_words(b):
             f_words[b] = keep.tile([P, PASSES, 2 * S], U8, name="f_words%d" % b, align_bytes=64)
@@ -80,67 +83,74 @@ def tile_downlink_leakage_rate_map_k7_kernel(
             nc.sync.dma_start(out=c_words[b][:].bitcast(I32), in_=leak_words[b].bitcast(I32))
 
         def load_scales(plane, src):
-            groups = src.shape[0]
-            for q in range(4):
+            passes = src.shape[0]
+            for q in range(QUADRANTS):
                 nc.sync.dma_start(
-                    out=plane[32 * q : 32 * q + 4, :].bitcast(I32).rearrange("r (g n) -> r g n", g=groups),
+                    out=plane[32 * q : 32 * q + 4, :].bitcast(I32).rearrange("r (g n) -> r g n", g=passes),
                     in_=src[:, 4 * q : 4 * q + 4, :].bitcast(I32).rearrange("g r n -> r g n"),
                 )
 
-        rows16 = keep.tile([P, P], BF16, name="rows16")
+        table16 = keep.tile([P, P], BF16, name="rows16")
         power_t = keep.tile([P, G, PACK], BF16, name="power_t")
-
         load_channel(0, 1)
         load_f_words(0)
         load_channel(1, 1)
-        load_scales(f_scales, precoder_scales)
-        load_channel(2, 1)
+        load_scales(f_scales_first, precoder_scales[0:PASSES])
         nc.sync.dma_start(out=power_t[:], in_=power.rearrange("b (p t) -> p b t", t=PACK))
-        nc.sync.dma_start(out=rows16[0:TILES, :], in_=noise.rearrange("b (i p) -> (b i) p", p=P))
-        nc.sync.dma_start(out=rows16[BW_ROW : BW_ROW + G * PACK, :], in_=bandwidth.rearrange("b (c p) -> (b c) p", p=P))
+        nc.sync.dma_start(out=table16[0:BW_FIRST, :], in_=noise.rearrange("b (i p) -> (b i) p", p=P))
+        nc.sync.dma_start(out=table16[BW_FIRST:TABLE_ROWS, :], in_=bandwidth.rearrange("b (c p) -> (b c) p", p=P))
+        for i in range(2, LOAD_TILES):
+            load_channel(i, 1)
         load_c_words(0)
         load_scales(c_scales, leak_scales)
-        load_channel(3, 1)
-        for first in range(4, TILES, 4):
-            load_channel(first, 4)
-            if first % TILES_PER_CELL == 4 and first // TILES_PER_CELL + 1 < G:
-                load_f_words(first // TILES_PER_CELL + 1)
-                load_c_words(first // TILES_PER_CELL + 1)
+        for first in range(LOAD_TILES, TILES, LOAD_TILES):
+            load_channel(first, LOAD_TILES)
+            if first == LOAD_TILES:
+                load_scales(f_scales_rest, precoder_scales[PASSES:])
+            next_cell, place = divmod(first + LOAD_TILES, TILES_PER_CELL)
+            if place == 0 and next_cell < G:
+                load_f_words(next_cell)
+                load_c_words(next_cell)
 
-        cols = keep.tile([P, 64], F32, name="cols")
-        inv_noise = keep.tile([P, TILES], F32, name="inv_noise")
-        unit = keep.tile([P, TILES], F32, name="unit")
+        cols = keep.tile([P, TABLE_ROWS], F32, name="cols")
+        ln_scale = keep.tile([P, TILES], F32, name="inv_noise")
+        ln_bias = keep.tile([P, TILES], F32, name="unit")
         safe_noise = keep.tile([P, TILES], F32, name="safe_noise")
 
-        def columns():
-            nc.vector.tensor_copy(out=rows32[0:TILES, :], in_=rows16[0:TILES, :])
-            nc.vector.tensor_copy(out=rows32[BW_ROW : BW_ROW + G * PACK, :], in_=rows16[BW_ROW : BW_ROW + G * PACK, :])
+        def turn_table():
+            nc.vector.tensor_copy(out=table32[0:BW_FIRST, :], in_=table16[0:BW_FIRST, :])
+            nc.vector.tensor_copy(out=table32[BW_FIRST:TABLE_ROWS, :], in_=table16[BW_FIRST:TABLE_ROWS, :])
             bank = psum.tile([P, P], F32, name="cols_bank", tag="bw_bank")
-            nc.tensor.transpose(bank[:], rows32[:], ident[:])
-            nc.vector.tensor_copy(out=cols[:], in_=bank[:, 0:64])
+            nc.tensor.transpose(bank[:], table32[:], ident[:])
+            nc.vector.tensor_copy(out=cols[:], in_=bank[:, 0:TABLE_ROWS])
+            noise_cols = cols[:, 0:TILES]
             nc.vector.scalar_tensor_tensor(
-                out=safe_noise[:], in0=cols[:, 0:TILES], scalar=0.0, in1=cols[:, 0:TILES], op0=ALU.is_equal, op1=ALU.add
+                out=safe_noise[:], in0=noise_cols, scalar=0.0, in1=noise_cols, op0=ALU.is_equal, op1=ALU.add
             )
-            nc.vector.reciprocal(out=inv_noise[:], in_=safe_noise[:])
-            nc.vector.tensor_tensor(out=unit[:], in0=cols[:, 0:TILES], in1=inv_noise[:], op=ALU.mult)
+            nc.vector.reciprocal(out=ln_scale[:], in_=safe_noise[:])
+            nc.vector.tensor_tensor(out=ln_bias[:], in0=noise_cols, in1=ln_scale[:], op=ALU.mult)
 
         ct_bank, chan_grouped, chan_codes, chan_scales = {}, {}, {}, {}
         e_bank, e2, et_bank, r_grouped, r_codes, r_scales = {}, {}, {}, {}, {}, {}
-        l_bank, log_den, num, log_num, diff, y, y16 = {}, {}, {}, {}, {}, {}, {}
-        l_twin = {}
-        yt_bank, y_grouped, y_codes, y_scales, bw_bank = {}, {}, {}, {}, {}
+        l_bank, l_twin, log_den, num, log_num, diff, bw_bank, y = {}, {}, {}, {}, {}, {}, {}, {}
+        y16, yt_bank, y_grouped, y_scales = {}, {}, {}, {}
 
         def transpose_channel(i):
-            tag = "yt_bank" if i % 2 == 1 and i < 7 else "ct_bank"
+            tag = "yt_bank" if i % 2 == 1 and i + lag[copy_channel] < lag[transpose_rate] else "ct_bank"
             ct_bank[i] = psum.tile([P, PASSES, 2, P], F32, name="ct_bank", tag=tag)
-            words = chan[i].bitcast(F32)
+            pairs = chan[i].bitcast(F32)
             for g in range(PASSES):
                 for h in range(2):
-                    nc.tensor.transpose(ct_bank[i][:, g, h, :], words[:, 256 * g + h : 256 * (g + 1) : 2], ident[:])
+                    nc.tensor.transpose(
+                        ct_bank[i][:, g, h, :], pairs[:, PASS_PAIRS * g + h : PASS_PAIRS * (g + 1) : 2], ident[:]
+                    )
 
         def copy_channel(i):
             chan_grouped[i] = work.tile([P, PASSES, P, 2], F32, name="chan_grouped", align_bytes=64)
-            nc.scalar.copy(out=chan_grouped[i][:], in_=ct_bank[i][:].rearrange("p g h u -> p g u h"))
+            nc.scalar.copy(
+                out=chan_grouped[i][:].rearrange("p g (v e) h -> p g v h e", e=2),
+                in_=ct_bank[i][:].rearrange("p g h (v e) -> p g v h e", e=2),
+            )
 
         def quantize_channel(i):
             chan_codes[i] = work.tile([P, PASSES * P], U32, name="chan_codes", align_bytes=64)
@@ -155,13 +165,13 @@ def tile_downlink_leakage_rate_map_k7_kernel(
             b = i // TILES_PER_CELL
             e_bank[i] = psum.tile([P, S], F32, name="e_bank")
             for g in range(PASSES):
-                group = PASSES * b + g
+                plane, place = (f_scales_first, g) if b == 0 else (f_scales_rest, PASSES * (b - 1) + g)
                 nc.tensor.matmul_mx(
                     out=e_bank[i][:],
                     lhsT=chan_codes[i][:, g * P : (g + 1) * P].bitcast(FP8X4),
                     lhsT_scale=chan_scales[i][:, g * P : (g + 1) * P],
                     rhs=f_words[b][:, g, :].bitcast(FP4X4),
-                    rhs_scale=f_scales[:, group * S : (group + 1) * S],
+                    rhs_scale=plane[:, place * S : (place + 1) * S],
                     start=(g == 0),
                     stop=(g == PASSES - 1),
                 )
@@ -183,9 +193,9 @@ def tile_downlink_leakage_rate_map_k7_kernel(
             b = i // TILES_PER_CELL
             r_grouped[i] = work.tile([P, P, PACK], BF16, name="r_grouped", align_bytes=64)
             nc.vector.tensor_tensor(
-                out=r_grouped[i][:],
-                in0=et_bank[i][:].rearrange("p t u -> p u t"),
-                in1=power_t[:, b, :].unsqueeze(1).to_broadcast([P, P, PACK]),
+                out=r_grouped[i][:].rearrange("p (v e) t -> p v t e", e=2),
+                in0=et_bank[i][:].rearrange("p t (v e) -> p v t e", e=2),
+                in1=power_t[:, b, :].unsqueeze(1).unsqueeze(3).to_broadcast([P, P // 2, PACK, 2]),
                 op=ALU.mult,
             )
 
@@ -214,7 +224,7 @@ def tile_downlink_leakage_rate_map_k7_kernel(
         def log_denominator(i):
             log_den[i] = work.tile([P, S], F32, name="log_den")
             nc.scalar.activation(
-                out=log_den[i][:], in_=l_bank[i][:], func=ACT.Ln, scale=inv_noise[:, i : i + 1], bias=unit[:, i : i + 1]
+                out=log_den[i][:], in_=l_bank[i][:], func=ACT.Ln, scale=ln_scale[:, i : i + 1], bias=ln_bias[:, i : i + 1]
             )
 
         def numerator(i):
@@ -232,19 +242,24 @@ def tile_downlink_leakage_rate_map_k7_kernel(
                 out=log_num[i][:].rearrange("u (c e t) -> u c e t", e=2, t=PACK),
                 in_=num[i][:].rearrange("u c t e -> u c e t"),
                 func=ACT.Ln,
-                scale=inv_noise[:, i : i + 1],
-                bias=unit[:, i : i + 1],
+                scale=ln_scale[:, i : i + 1],
+                bias=ln_bias[:, i : i + 1],
             )
 
-        def difference(i):
+        def difference(i, engine=nc.gpsimd):
             diff[i] = work.tile([P, S], F32, name="diff")
-            nc.gpsimd.tensor_tensor(out=diff[i][:], in0=log_num[i][:], in1=log_den[i][:], op=ALU.subtract)
+            engine.tensor_tensor(out=diff[i][:], in0=log_num[i][:], in1=log_den[i][:], op=ALU.subtract)
 
         def spread_bandwidth(b):
-            bw_bank[b] = psum.tile([P, PACK, P], F32, name="bw_bank", tag="bw_bank")
-            for c in range(PACK):
-                col = BW_ROW + PACK * b + c
+            bw_bank[b] = psum.tile([P, BW_CHUNKS, P], F32, name="bw_bank", tag="bw_bank")
+            for c in range(BW_CHUNKS):
+                col = BW_FIRST + BW_CHUNKS * b + c
                 nc.tensor.transpose(bw_bank[b][:, c, :], cols[:, col : col + 1].to_broadcast([P, P]), ident[:])
+
+        def next_bandwidth(i):
+            next_cell, place = divmod(i + 1, TILES_PER_CELL)
+            if place == 0 and next_cell < G:
+                spread_bandwidth(next_cell)
 
         def rate(i):
             b = i // TILES_PER_CELL
@@ -256,73 +271,97 @@ def tile_downlink_leakage_rate_map_k7_kernel(
             y16[i] = work.tile([P, 2, P, 2], BF16, name="y16")
             nc.vector.tensor_copy(out=y16[i][:], in_=y[i][:].rearrange("u (p h e) -> u h p e", h=2, e=2))
 
-        def transpose_rate(i):
-            yt_bank[i] = psum.tile([P, 2, P], F32, name="yt_bank", tag="yt_bank")
-            words = y16[i][:].rearrange("u h p e -> u (h p e)").bitcast(F32)
+        def transpose_rate(i, tag="yt_bank"):
+            yt_bank[i] = psum.tile([P, 2, P], F32, name="yt_bank", tag=tag)
+            pairs = y16[i][:].rearrange("u h p e -> u (h p e)").bitcast(F32)
             for h in range(2):
-                nc.tensor.transpose(yt_bank[i][:, h, :], words[:, h * P : (h + 1) * P], ident[:])
+                nc.tensor.transpose(yt_bank[i][:, h, :], pairs[:, h * P : (h + 1) * P], ident[:])
 
         def copy_rate(i):
-            pair, half = divmod(i, 2)
+            twin, half = divmod(i, 2)
             if half == 0:
-                y_grouped[pair] = work.tile([P, 2, P, 2], F32, name="y_grouped", align_bytes=64)
-            nc.scalar.copy(out=y_grouped[pair][:, half], in_=yt_bank[i][:].rearrange("p h u -> p u h"))
+                y_grouped[twin] = work.tile([P, 2, P, 2], F32, name="y_grouped", align_bytes=64)
+            nc.scalar.copy(
+                out=y_grouped[twin][:, half].rearrange("p (v e) h -> p v h e", e=2),
+                in_=yt_bank[i][:].rearrange("p h (v e) -> p v h e", e=2),
+            )
 
         def quantize_rate(i):
             if i % 2 == 0:
                 return
             first = i - 1
-            group, slot = divmod(first, CODE_GROUP)
             b, place = divmod(first, TILES_PER_CELL)
-            if slot == 0:
-                y_codes[group] = keep.tile([P, CODE_GROUP * P], U32, name="y_codes%d" % group, align_bytes=64)
+            y_codes = keep.tile([P, 2 * P], U32, name="y_codes%d" % first, align_bytes=64)
             if place == 0:
                 y_scales[b] = keep.tile([P, U], U8, name="y_scales%d" % b, align_bytes=64)
             nc.vector.quantize_mx(
-                out=y_codes[group][:, slot * P : (slot + 2) * P].bitcast(FP8X4),
+                out=y_codes[:].bitcast(FP8X4),
                 scales=y_scales[b][:, place * P : (place + 2) * P],
                 in_=y_grouped[first // 2][:].rearrange("p n u h -> p (n u h)").bitcast(BF16),
             )
-            if slot + 2 == CODE_GROUP:
-                width = CODE_GROUP * P
-                nc.sync.dma_start(out=code_rows[:, group * width : (group + 1) * width], in_=y_codes[group][:].bitcast(I32))
+            nc.sync.dma_start(out=code_rows[:, first * P : (first + 2) * P], in_=y_codes[:].bitcast(I32))
             if place + 2 == TILES_PER_CELL:
-                for q in range(4):
-                    nc.sync.dma_start(
+                queue = nc.scalar if b == G - 1 else nc.sync
+                for q in range(QUADRANTS):
+                    queue.dma_start(
                         out=scale_rows[4 * q : 4 * q + 4, b * U // 4 : (b + 1) * U // 4],
                         in_=y_scales[b][32 * q : 32 * q + 4, :].bitcast(I32),
                     )
 
-        def next_bandwidth(i):
-            if (i + 1) % TILES_PER_CELL == 0 and i + 1 < TILES:
-                spread_bandwidth((i + 1) // TILES_PER_CELL)
-
-        stages = [
-            (leakage, 5),
-            (square, 3),
-            (log_denominator, 5),
-            (difference, 6),
-            (rate, 7),
-            (received, 4),
-            (numerator, 5),
-            (transpose_rate, 8),
-            (next_bandwidth, 7),
-            (transpose_square, 3),
-            (amplitude, 2),
-            (copy_channel, 1),
-            (transpose_channel, 0),
-            (copy_rate, 8),
-            (log_numerator, 5),
-            (quantize_received, 4),
-            (round_rate, 7),
-            (quantize_rate, 8),
-            (quantize_channel, 1),
+        pipeline = [
+            [transpose_channel],
+            [copy_channel, quantize_channel],
+            [amplitude],
+            [square, transpose_square],
+            [received, quantize_received],
+            [leakage, log_denominator, numerator, log_numerator],
+            [difference],
+            [rate, next_bandwidth, round_rate],
+            [transpose_rate, copy_rate, quantize_rate],
         ]
-        for step in range(TILES + 8):
-            for stage, lag in stages:
-                if 0 <= step - lag < TILES:
-                    stage(step - lag)
-            if step == 2:
-                columns()
-            if step == 4:
+        lag = {stage: n for n, group in enumerate(pipeline) for stage in group}
+
+        step_order = [
+            leakage,
+            square,
+            log_denominator,
+            difference,
+            rate,
+            received,
+            numerator,
+            transpose_rate,
+            next_bandwidth,
+            transpose_square,
+            amplitude,
+            copy_channel,
+            transpose_channel,
+            copy_rate,
+            log_numerator,
+            quantize_received,
+            round_rate,
+            quantize_rate,
+            quantize_channel,
+        ]
+        last = TILES - 1
+        for step in range(last + lag[difference]):
+            for stage in step_order:
+                if 0 <= step - lag[stage] < TILES:
+                    stage(step - lag[stage])
+            if step == lag[amplitude]:
+                turn_table()
+            if step == lag[leakage] - 1:
                 spread_bandwidth(0)
+
+        rate(last - 1)
+        difference(last, nc.vector)
+        transpose_rate(last - 2)
+        copy_rate(last - 2)
+        round_rate(last - 1)
+        rate(last)
+        transpose_rate(last - 1, "ct_bank")
+        copy_rate(last - 1)
+        quantize_rate(last - 2)
+        round_rate(last)
+        transpose_rate(last)
+        copy_rate(last)
+        quantize_rate(last)

from contextlib import ExitStack

import concourse.mybir as mybir
from concourse.masks import make_identity

G, U, K, S = 4, 1024, 1024, 512
FLOPS = 2 * G * U * S * (K + S)

F32 = mybir.dt.float32
BF16 = mybir.dt.bfloat16
I32 = mybir.dt.int32
U32 = mybir.dt.uint32
U8 = mybir.dt.uint8
FP8X4 = mybir.dt.float8_e4m3fn_x4
FP4X4 = mybir.dt.float4_e2m1fn_x4
ALU = mybir.AluOpType
ACT = mybir.ActivationFunctionType

P = 128
PACK = 4
K_PASS = P * PACK
PASSES = K // K_PASS
PASS_PAIRS = K_PASS // 2
QUADRANTS = 4
TILES = G * U // P
TILES_PER_CELL = U // P
LOAD_TILES = 4
BW_CHUNKS = S // P
BW_FIRST = TILES
TABLE_ROWS = BW_FIRST + G * BW_CHUNKS


def tile_downlink_leakage_rate_map_k7_kernel(
    tc, channel, precoder_words, precoder_scales, leak_words, leak_scales, power, noise, bandwidth, out_0, out_1, out_2
):
    nc = tc.nc
    channel_rows = channel.rearrange("b u k -> (b u) k")
    y_rows = out_0.rearrange("b u j -> (b u) j")
    code_rows = out_1.rearrange("g p m t -> (g p) (m t)").bitcast(I32)
    scale_rows = out_2.rearrange("g q m -> (g q) m").bitcast(I32)

    with ExitStack() as ctx:
        keep = ctx.enter_context(tc.tile_pool(name="keep", bufs=1))
        work = ctx.enter_context(tc.tile_pool(name="work", bufs=3))
        psum = ctx.enter_context(tc.psum_pool(name="psum", bufs=1))
        ctx.enter_context(tc.manual_schedule())

        ident = keep.tile([P, P], F32, name="ident")
        make_identity(nc, ident[:])

        f_scales_first = keep.tile([P, PASSES * S], U8, name="f_scales_first", align_bytes=64)
        f_scales_rest = keep.tile([P, (G - 1) * PASSES * S], U8, name="f_scales_rest", align_bytes=64)
        c_scales = keep.tile([P, G * S], U8, name="c_scales", align_bytes=64)
        warm = keep.tile([P, 8], F32, name="warm")
        table32 = keep.tile([P, P], F32, name="rows32")
        nc.vector.memset(warm[:], 1.0)
        nc.vector.memset(f_scales_first[:].bitcast(I32), 0)
        nc.vector.memset(c_scales[:].bitcast(I32), 0)
        nc.vector.memset(f_scales_rest[:].bitcast(I32), 0)
        nc.vector.memset(table32[:], 0.0)
        warm_out = keep.tile([P, 8], F32, name="warm_out")
        nc.scalar.activation(out=warm_out[:], in_=warm[:], func=ACT.Ln)

        chan, f_words, c_words = {}, {}, {}

        def load_channel(first, count):
            rows = keep.tile([P, count, K], BF16, name="chan%d" % first)
            nc.sync.dma_start(
                out=rows[:], in_=channel_rows[first * P : (first + count) * P, :].rearrange("(n u) k -> u n k", u=P)
            )
            for n in range(count):
                chan[first + n] = rows[:, n, :]

        def load_f_words(b):
            f_words[b] = keep.tile([P, PASSES, 2 * S], U8, name="f_words%d" % b, align_bytes=64)
            nc.sync.dma_start(
                out=f_words[b][:].bitcast(I32),
                in_=precoder_words[PASSES * b : PASSES * (b + 1)].bitcast(I32).rearrange("g p n -> p g n"),
            )

        def load_c_words(b):
            c_words[b] = keep.tile([P, 2 * S], U8, name="c_words%d" % b, align_bytes=64)
            nc.sync.dma_start(out=c_words[b][:].bitcast(I32), in_=leak_words[b].bitcast(I32))

        def load_scales(plane, src):
            passes = src.shape[0]
            for q in range(QUADRANTS):
                nc.sync.dma_start(
                    out=plane[32 * q : 32 * q + 4, :].bitcast(I32).rearrange("r (g n) -> r g n", g=passes),
                    in_=src[:, 4 * q : 4 * q + 4, :].bitcast(I32).rearrange("g r n -> r g n"),
                )

        table16 = keep.tile([P, P], BF16, name="rows16")
        power_t = keep.tile([P, G, PACK], BF16, name="power_t")
        load_channel(0, 1)
        load_f_words(0)
        load_channel(1, 1)
        load_scales(f_scales_first, precoder_scales[0:PASSES])
        nc.sync.dma_start(out=power_t[:], in_=power.rearrange("b (p t) -> p b t", t=PACK))
        nc.sync.dma_start(out=table16[0:BW_FIRST, :], in_=noise.rearrange("b (i p) -> (b i) p", p=P))
        nc.sync.dma_start(out=table16[BW_FIRST:TABLE_ROWS, :], in_=bandwidth.rearrange("b (c p) -> (b c) p", p=P))
        for i in range(2, LOAD_TILES):
            load_channel(i, 1)
        load_c_words(0)
        load_scales(c_scales, leak_scales)
        for first in range(LOAD_TILES, TILES, LOAD_TILES):
            load_channel(first, LOAD_TILES)
            if first == LOAD_TILES:
                load_scales(f_scales_rest, precoder_scales[PASSES:])
            next_cell, place = divmod(first + LOAD_TILES, TILES_PER_CELL)
            if place == 0 and next_cell < G:
                load_f_words(next_cell)
                load_c_words(next_cell)

        cols = keep.tile([P, TABLE_ROWS], F32, name="cols")
        ln_scale = keep.tile([P, TILES], F32, name="inv_noise")
        ln_bias = keep.tile([P, TILES], F32, name="unit")
        safe_noise = keep.tile([P, TILES], F32, name="safe_noise")

        def turn_table():
            nc.vector.tensor_copy(out=table32[0:BW_FIRST, :], in_=table16[0:BW_FIRST, :])
            nc.vector.tensor_copy(out=table32[BW_FIRST:TABLE_ROWS, :], in_=table16[BW_FIRST:TABLE_ROWS, :])
            bank = psum.tile([P, P], F32, name="cols_bank", tag="bw_bank")
            nc.tensor.transpose(bank[:], table32[:], ident[:])
            nc.vector.tensor_copy(out=cols[:], in_=bank[:, 0:TABLE_ROWS])
            noise_cols = cols[:, 0:TILES]
            nc.vector.scalar_tensor_tensor(
                out=safe_noise[:], in0=noise_cols, scalar=0.0, in1=noise_cols, op0=ALU.is_equal, op1=ALU.add
            )
            nc.vector.reciprocal(out=ln_scale[:], in_=safe_noise[:])
            nc.vector.tensor_tensor(out=ln_bias[:], in0=noise_cols, in1=ln_scale[:], op=ALU.mult)

        ct_bank, chan_grouped, chan_codes, chan_scales = {}, {}, {}, {}
        e_bank, e2, et_bank, r_grouped, r_codes, r_scales = {}, {}, {}, {}, {}, {}
        l_bank, l_twin, log_den, num, log_num, diff, bw_bank, y = {}, {}, {}, {}, {}, {}, {}, {}
        y16, yt_bank, y_grouped, y_scales = {}, {}, {}, {}

        def transpose_channel(i):
            tag = "yt_bank" if i % 2 == 1 and i + lag[copy_channel] < lag[transpose_rate] else "ct_bank"
            ct_bank[i] = psum.tile([P, PASSES, 2, P], F32, name="ct_bank", tag=tag)
            pairs = chan[i].bitcast(F32)
            for g in range(PASSES):
                for h in range(2):
                    nc.tensor.transpose(
                        ct_bank[i][:, g, h, :], pairs[:, PASS_PAIRS * g + h : PASS_PAIRS * (g + 1) : 2], ident[:]
                    )

        def copy_channel(i):
            chan_grouped[i] = work.tile([P, PASSES, P, 2], F32, name="chan_grouped", align_bytes=64)
            nc.scalar.copy(
                out=chan_grouped[i][:].rearrange("p g (v e) h -> p g v h e", e=2),
                in_=ct_bank[i][:].rearrange("p g h (v e) -> p g v h e", e=2),
            )

        def quantize_channel(i):
            chan_codes[i] = work.tile([P, PASSES * P], U32, name="chan_codes", align_bytes=64)
            chan_scales[i] = work.tile([P, PASSES * P], U8, name="chan_scales", align_bytes=64)
            nc.vector.quantize_mx(
                out=chan_codes[i][:].bitcast(FP8X4),
                scales=chan_scales[i][:],
                in_=chan_grouped[i][:].rearrange("p g u h -> p (g u h)").bitcast(BF16),
            )

        def amplitude(i):
            b = i // TILES_PER_CELL
            e_bank[i] = psum.tile([P, S], F32, name="e_bank")
            for g in range(PASSES):
                plane, place = (f_scales_first, g) if b == 0 else (f_scales_rest, PASSES * (b - 1) + g)
                nc.tensor.matmul_mx(
                    out=e_bank[i][:],
                    lhsT=chan_codes[i][:, g * P : (g + 1) * P].bitcast(FP8X4),
                    lhsT_scale=chan_scales[i][:, g * P : (g + 1) * P],
                    rhs=f_words[b][:, g, :].bitcast(FP4X4),
                    rhs_scale=plane[:, place * S : (place + 1) * S],
                    start=(g == 0),
                    stop=(g == PASSES - 1),
                )

        def square(i):
            e2[i] = work.tile([P, PACK, P], F32, name="e2", bufs=5)
            nc.scalar.activation(
                out=e2[i][:].rearrange("u t (c n) -> u c t n", n=4),
                in_=e_bank[i][:].rearrange("u (c n t) -> u c t n", n=4, t=PACK),
                func=ACT.Square,
            )

        def transpose_square(i):
            et_bank[i] = psum.tile([P, PACK, P], F32, name="et_bank", bufs=2)
            for t in range(PACK):
                nc.tensor.transpose(et_bank[i][:, t, :], e2[i][:, t, :], ident[:])

        def received(i):
            b = i // TILES_PER_CELL
            r_grouped[i] = work.tile([P, P, PACK], BF16, name="r_grouped", align_bytes=64)
            nc.vector.tensor_tensor(
                out=r_grouped[i][:].rearrange("p (v e) t -> p v t e", e=2),
                in0=et_bank[i][:].rearrange("p t (v e) -> p v t e", e=2),
                in1=power_t[:, b, :].unsqueeze(1).unsqueeze(3).to_broadcast([P, P // 2, PACK, 2]),
                op=ALU.mult,
            )

        def quantize_received(i):
            r_codes[i] = work.tile([P, P], U32, name="r_codes", align_bytes=64)
            r_scales[i] = work.tile([P, P], U8, name="r_scales", align_bytes=64)
            nc.vector.quantize_mx(
                out=r_codes[i][:].bitcast(FP8X4), scales=r_scales[i][:], in_=r_grouped[i][:].rearrange("p u t -> p (u t)")
            )

        def leakage(i):
            b = i // TILES_PER_CELL
            l_bank[i] = psum.tile([P, S], F32, name="l_bank")
            l_twin[i] = psum.tile([P, S], F32, name="l_twin")
            for bank in (l_bank[i], l_twin[i]):
                nc.tensor.matmul_mx(
                    out=bank[:],
                    lhsT=r_codes[i][:].bitcast(FP8X4),
                    lhsT_scale=r_scales[i][:],
                    rhs=c_words[b][:].bitcast(FP4X4),
                    rhs_scale=c_scales[:, b * S : (b + 1) * S],
                    start=True,
                    stop=True,
                )

        def log_denominator(i):
            log_den[i] = work.tile([P, S], F32, name="log_den")
            nc.scalar.activation(
                out=log_den[i][:], in_=l_bank[i][:], func=ACT.Ln, scale=ln_scale[:, i : i + 1], bias=ln_bias[:, i : i + 1]
            )

        def numerator(i):
            num[i] = work.tile([P, P // 2, PACK, 2], F32, name="num")
            nc.vector.tensor_tensor(
                out=num[i][:],
                in0=l_twin[i][:].rearrange("u (c e t) -> u c t e", e=2, t=PACK),
                in1=e2[i][:].rearrange("u t (c e) -> u c t e", e=2),
                op=ALU.add,
            )

        def log_numerator(i):
            log_num[i] = work.tile([P, S], F32, name="log_num")
            nc.scalar.activation(
                out=log_num[i][:].rearrange("u (c e t) -> u c e t", e=2, t=PACK),
                in_=num[i][:].rearrange("u c t e -> u c e t"),
                func=ACT.Ln,
                scale=ln_scale[:, i : i + 1],
                bias=ln_bias[:, i : i + 1],
            )

        def difference(i, engine=nc.gpsimd):
            diff[i] = work.tile([P, S], F32, name="diff")
            engine.tensor_tensor(out=diff[i][:], in0=log_num[i][:], in1=log_den[i][:], op=ALU.subtract)

        def spread_bandwidth(b):
            bw_bank[b] = psum.tile([P, BW_CHUNKS, P], F32, name="bw_bank", tag="bw_bank")
            for c in range(BW_CHUNKS):
                col = BW_FIRST + BW_CHUNKS * b + c
                nc.tensor.transpose(bw_bank[b][:, c, :], cols[:, col : col + 1].to_broadcast([P, P]), ident[:])

        def next_bandwidth(i):
            next_cell, place = divmod(i + 1, TILES_PER_CELL)
            if place == 0 and next_cell < G:
                spread_bandwidth(next_cell)

        def rate(i):
            b = i // TILES_PER_CELL
            y[i] = work.tile([P, S], F32, name="y", bufs=TILES)
            nc.vector.tensor_tensor(out=y[i][:], in0=diff[i][:], in1=bw_bank[b][:].rearrange("u c p -> u (c p)"), op=ALU.mult)
            nc.sync.dma_start(out=y_rows[i * P : (i + 1) * P, :], in_=y[i][:])

        def round_rate(i):
            y16[i] = work.tile([P, 2, P, 2], BF16, name="y16")
            nc.vector.tensor_copy(out=y16[i][:], in_=y[i][:].rearrange("u (p h e) -> u h p e", h=2, e=2))

        def transpose_rate(i, tag="yt_bank"):
            yt_bank[i] = psum.tile([P, 2, P], F32, name="yt_bank", tag=tag)
            pairs = y16[i][:].rearrange("u h p e -> u (h p e)").bitcast(F32)
            for h in range(2):
                nc.tensor.transpose(yt_bank[i][:, h, :], pairs[:, h * P : (h + 1) * P], ident[:])

        def copy_rate(i):
            twin, half = divmod(i, 2)
            if half == 0:
                y_grouped[twin] = work.tile([P, 2, P, 2], F32, name="y_grouped", align_bytes=64)
            nc.scalar.copy(
                out=y_grouped[twin][:, half].rearrange("p (v e) h -> p v h e", e=2),
                in_=yt_bank[i][:].rearrange("p h (v e) -> p v h e", e=2),
            )

        def quantize_rate(i):
            if i % 2 == 0:
                return
            first = i - 1
            b, place = divmod(first, TILES_PER_CELL)
            y_codes = keep.tile([P, 2 * P], U32, name="y_codes%d" % first, align_bytes=64)
            if place == 0:
                y_scales[b] = keep.tile([P, U], U8, name="y_scales%d" % b, align_bytes=64)
            nc.vector.quantize_mx(
                out=y_codes[:].bitcast(FP8X4),
                scales=y_scales[b][:, place * P : (place + 2) * P],
                in_=y_grouped[first // 2][:].rearrange("p n u h -> p (n u h)").bitcast(BF16),
            )
            nc.sync.dma_start(out=code_rows[:, first * P : (first + 2) * P], in_=y_codes[:].bitcast(I32))
            if place + 2 == TILES_PER_CELL:
                queue = nc.scalar if b == G - 1 else nc.sync
                for q in range(QUADRANTS):
                    queue.dma_start(
                        out=scale_rows[4 * q : 4 * q + 4, b * U // 4 : (b + 1) * U // 4],
                        in_=y_scales[b][32 * q : 32 * q + 4, :].bitcast(I32),
                    )

        pipeline = [
            [transpose_channel],
            [copy_channel, quantize_channel],
            [amplitude],
            [square, transpose_square],
            [received, quantize_received],
            [leakage, log_denominator, numerator, log_numerator],
            [difference],
            [rate, next_bandwidth, round_rate],
            [transpose_rate, copy_rate, quantize_rate],
        ]
        lag = {stage: n for n, group in enumerate(pipeline) for stage in group}

        step_order = [
            leakage,
            square,
            log_denominator,
            difference,
            rate,
            received,
            numerator,
            transpose_rate,
            next_bandwidth,
            transpose_square,
            amplitude,
            copy_channel,
            transpose_channel,
            copy_rate,
            log_numerator,
            quantize_received,
            round_rate,
            quantize_rate,
            quantize_channel,
        ]
        last = TILES - 1
        for step in range(last + lag[difference]):
            for stage in step_order:
                if 0 <= step - lag[stage] < TILES:
                    stage(step - lag[stage])
            if step == lag[amplitude]:
                turn_table()
            if step == lag[leakage] - 1:
                spread_bandwidth(0)

        rate(last - 1)
        difference(last, nc.vector)
        transpose_rate(last - 2)
        copy_rate(last - 2)
        round_rate(last - 1)
        rate(last)
        transpose_rate(last - 1, "ct_bank")
        copy_rate(last - 1)
        quantize_rate(last - 2)
        round_rate(last)
        transpose_rate(last)
        copy_rate(last)
        quantize_rate(last)
